import numpy as np, ml_dtypes
CORES = [6,14,22,30,38,134,142,150,158]
N = 9
F = 128
def setup_inputs(rng):
    return {"ah": rng.standard_normal((N, 128, 128), dtype=np.float32).astype(ml_dtypes.bfloat16), "al": (rng.standard_normal((N, 128, 128), dtype=np.float32) / 256).astype(ml_dtypes.bfloat16), "bh": rng.standard_normal((N, 128, F), dtype=np.float32).astype(ml_dtypes.bfloat16), "bl": (rng.standard_normal((N, 128, F), dtype=np.float32) / 256).astype(ml_dtypes.bfloat16)}
def setup_inputs_big(rng):
    d = setup_inputs(rng)
    for k in ("ah", "al", "bh", "bl"): d[k] = (d[k].astype(np.float32) * 1024.0).astype(d[k].dtype)
    return d
def setup_inputs_small(rng):
    d = setup_inputs(rng)
    for k in ("ah", "al", "bh", "bl"): d[k] = (d[k].astype(np.float32) * (1 / 1024.0)).astype(d[k].dtype)
    return d
def setup_inputs_apart(rng):
    d = setup_inputs(rng)
    f = (10.0 ** rng.permutation(np.linspace(-1.5, 1.5, N))).astype(np.float32).reshape(N, 1, 1)
    for k in ("ah", "al", "bh", "bl"): d[k] = (d[k].astype(np.float32) * f).astype(d[k].dtype)
    return d
def reference(ah, al, bh, bl):
    AH, AL, BH, BL = ah.astype(np.float64), al.astype(np.float64), bh.astype(np.float64), bl.astype(np.float64)
    s = sum((AH[j] + AL[j]).T @ (BH[j] + BL[j]) for j in range(N))
    s = s.astype(np.float32 if ah.dtype != np.float64 else np.float64)
    return {"y": np.broadcast_to(s, (N,) + s.shape)}

@@ -1,0 +1,97 @@
+import comms_topo
+from concourse.bass import DstId, RemoteDMATransfer
+
+CORES = [6, 14, 22, 30, 38, 134, 142, 150, 158]
+D = 128
+
+
+def _pairs(cores, topo):
+    return [(a, b) for i, a in enumerate(cores) for b in cores[i + 1:] if topo.mates(a, b)]
+
+
+K = len(_pairs(CORES, comms_topo))
+W = D // K
+
+SCRATCH = {
+    "sah": ("sbuf", [D, D], "bfloat16"),
+    "sal": ("sbuf", [D, D], "bfloat16"),
+    "sbh": ("sbuf", [D, D], "bfloat16"),
+    "sbl": ("sbuf", [D, D], "bfloat16"),
+    "acc": ("psum", [D, D], "float32"),
+    "p": ("sbuf", [D, D], "float32"),
+    "stage": ("dram", [K, D, W], "float32"),
+    "land": ("dram", [len(CORES) - 1, D, W], "float32"),
+    "res": ("dram", [K, D, W], "float32"),
+}
+SEMAPHORES = ["ldh", "ldl", "mm", "cp", "staged", "arr", "sent", "got", "done"]
+
+
+def rank_program(g, core, T, topo):
+    rank = T.rank_of(core)
+    if rank is None:
+        return
+    S = T.sem
+    cores = list(T.cores)
+    others = [c for c in cores if c != core]
+    pairs = _pairs(cores, topo)
+
+    def dst_id(d):
+        rid, pid = topo.addr(d, core)
+        return DstId(rid=rid, pnc=pid)
+
+    def slot(sender, receiver):
+        a, b = T.rank_of(sender), T.rank_of(receiver)
+        return a - (1 if a > b else 0)
+
+    allowed = topo.mask(core, others[0])
+    for d in others:
+        allowed &= topo.mask(core, d)
+    engines = [e for e in range(16) if (allowed >> e) & 1]
+    engines = engines[::len(engines) // K][:K]
+    all_mask = 0
+    for e in engines:
+        all_mask |= 1 << e
+
+    g.sync.dma_start(T.sah[:], T.ah[:]).then_inc(S.ldh, 16)
+    g.scalar.dma_start(T.sbh[:], T.bh[:]).then_inc(S.ldh, 16)
+    g.sync.dma_start(T.sal[:], T.al[:]).then_inc(S.ldl, 16)
+    g.scalar.dma_start(T.sbl[:], T.bl[:]).then_inc(S.ldl, 16)
+    g.tensor.wait_ge(S.ldh, 32)
+    g.tensor.matmul(T.acc[:], T.sah[:], T.sbh[:], True, False).then_inc(S.mm, 1)
+    g.tensor.wait_ge(S.ldl, 32)
+    g.tensor.matmul(T.acc[:], T.sah[:], T.sbl[:], False, False).then_inc(S.mm, 1)
+    g.tensor.matmul(T.acc[:], T.sal[:], T.sbh[:], False, False).then_inc(S.mm, 1)
+    g.tensor.matmul(T.acc[:], T.sal[:], T.sbl[:], False, True).then_inc(S.mm, 1)
+
+    g.vector.wait_ge(S.mm, 4)
+    g.vector.tensor_copy(T.p[:], T.acc[:]).then_inc(S.cp, 1)
+    g.sync.wait_ge(S.cp, 1)
+    g.sync.dma_start(T.stage[:], T.p[:]).then_inc(S.staged, 16)
+
+    g.wait_ge(S.staged, 16)
+    sent = 0
+    trs = []
+    mine = None
+    for s, pair in enumerate(pairs):
+        if core in pair:
+            mine = s
+        dsts = [d for d in pair if d != core]
+        trs.append(RemoteDMATransfer(dst_ids=[dst_id(d) for d in dsts], dma_engine_mask=1 << engines[s],
+                                     remote_sem=S.arr, srcs=[T.stage[s]],
+                                     dsts=[T.land[slot(core, d)] for d in dsts], alu_op=0))
+        sent += 1
+    g.remote_dma_fused(trs, local_sem=S.sent)
+
+    if mine is not None:
+        g.wait_ge(S.arr, len(others))
+        dsts = [d for d in others if topo.mates(core, d) or topo.same_plane(core, d)]
+        g.remote_dma_fused([RemoteDMATransfer(dst_ids=[dst_id(d) for d in dsts], dma_engine_mask=all_mask,
+                                              remote_sem=S.got,
+                                              srcs=[T.stage[mine]] + [T.land[i] for i in range(len(others))],
+                                              dsts=[T.res[mine] for d in dsts], alu_op=1)], local_sem=S.sent)
+        sent += len(engines)
+
+    g.sync.wait_ge(S.got, K * len(engines))
+    g.sync.dma_start(T.y[:], T.res[:]).then_inc(S.done, 16)
+    g.sync.wait_ge(S.done, 16)
+    g.wait_ge(S.sent, sent)

@@ -1,29 +1,39 @@
 import comms_topo
 from concourse.bass import DstId, RemoteDMATransfer
+from concourse.mybir import AluOpType
 
 CORES = [6, 14, 22, 30, 38, 134, 142, 150, 158]
 D = 128
 
 
-def _pairs(cores, topo):
-    return [(a, b) for i, a in enumerate(cores) for b in cores[i + 1:] if topo.mates(a, b)]
+def _owners(cores, topo):
+    return [a for a in cores if any(topo.mates(a, b) for b in cores)]
 
 
-K = len(_pairs(CORES, comms_topo))
-W = D // K
+NP = len(_owners(CORES, comms_topo))
+W = D // NP
+NO = len(CORES) - 1
 
 SCRATCH = {
     "sah": ("sbuf", [D, D], "bfloat16"),
     "sal": ("sbuf", [D, D], "bfloat16"),
     "sbh": ("sbuf", [D, D], "bfloat16"),
     "sbl": ("sbuf", [D, D], "bfloat16"),
-    "acc": ("psum", [D, D], "float32"),
+    "acc": ("psum", [D, 512], "float32"),
+    "acc2": ("psum", [D, 512], "float32"),
     "p": ("sbuf", [D, D], "float32"),
-    "stage": ("dram", [K, D, W], "float32"),
-    "land": ("dram", [len(CORES) - 1, D, W], "float32"),
-    "res": ("dram", [K, D, W], "float32"),
+    "stage": ("dram", [NP, D, W], "float32"),
+    "land": ("dram", [NO, D, W], "float32"),
+    "res": ("dram", [NP, D, W], "float32"),
+    "u": ("sbuf", [D, W + 1], "float32"),
+    "zdd": ("dram", [NO, W * (W + 1)], "float32"),
+    "sel": ("sbuf", [D, W], "float32"),
+    "lz": ("sbuf", [D, D], "float32"),
+    "own0": ("sbuf", [W, D], "float32"),
+    "ysl": ("sbuf", [W, D], "float32"),
 }
-SEMAPHORES = ["ldh", "ldl", "mm", "cp", "staged", "arr", "sent", "got", "done"]
+SEMAPHORES = ["ldh", "ldl", "mm", "cp", "staged", "arr", "sent", "got", "done",
+              "ms", "zs", "sels", "owns", "lzs", "sm", "ys", "doneo"]
 
 
 def rank_program(g, core, T, topo):
@@ -33,7 +43,8 @@ def rank_program(g, core, T, topo):
     S = T.sem
     cores = list(T.cores)
     others = [c for c in cores if c != core]
-    pairs = _pairs(cores, topo)
+    owners = _owners(cores, topo)
+    mine = owners.index(core) if core in owners else None
 
     def dst_id(d):
         rid, pid = topo.addr(d, core)
@@ -47,51 +58,74 @@ def rank_program(g, core, T, topo):
     for d in others:
         allowed &= topo.mask(core, d)
     engines = [e for e in range(16) if (allowed >> e) & 1]
-    engines = engines[::len(engines) // K][:K]
-    all_mask = 0
-    for e in engines:
-        all_mask |= 1 << e
 
     g.sync.dma_start(T.sah[:], T.ah[:]).then_inc(S.ldh, 16)
     g.scalar.dma_start(T.sbh[:], T.bh[:]).then_inc(S.ldh, 16)
     g.sync.dma_start(T.sal[:], T.al[:]).then_inc(S.ldl, 16)
     g.scalar.dma_start(T.sbl[:], T.bl[:]).then_inc(S.ldl, 16)
+    if mine is not None:
+        g.vector.memset(T.u[:], 0.0).then_inc(S.ms, 1)
+        g.vector.wait_ge(S.ms, 1)
+        g.vector.memset(T.u[:, 0:1], 1.0).then_inc(S.ms, 1)
+        g.scalar.wait_ge(S.ms, 2)
+        g.scalar.dma_start(T.zdd[:], T.u[:]).then_inc(S.zs, 16)
+        g.scalar.wait_ge(S.zs, 16)
+        g.scalar.dma_start(T.sel[:], T.zdd[:, 0:W * W]).then_inc(S.sels, 16)
     g.tensor.wait_ge(S.ldh, 32)
-    g.tensor.matmul(T.acc[:], T.sah[:], T.sbh[:], True, False).then_inc(S.mm, 1)
+    g.tensor.matmul(T.acc[:, 0:D], T.sah[:], T.sbh[:], True, False).then_inc(S.mm, 1)
     g.tensor.wait_ge(S.ldl, 32)
-    g.tensor.matmul(T.acc[:], T.sah[:], T.sbl[:], False, False).then_inc(S.mm, 1)
-    g.tensor.matmul(T.acc[:], T.sal[:], T.sbh[:], False, False).then_inc(S.mm, 1)
-    g.tensor.matmul(T.acc[:], T.sal[:], T.sbl[:], False, True).then_inc(S.mm, 1)
+    g.tensor.matmul(T.acc[:, 0:D], T.sah[:], T.sbl[:], False, False).then_inc(S.mm, 1)
+    g.tensor.matmul(T.acc[:, 0:D], T.sal[:], T.sbh[:], False, False).then_inc(S.mm, 1)
+    g.tensor.matmul(T.acc[:, 0:D], T.sal[:], T.sbl[:], False, True).then_inc(S.mm, 1)
 
     g.vector.wait_ge(S.mm, 4)
-    g.vector.tensor_copy(T.p[:], T.acc[:]).then_inc(S.cp, 1)
+    g.vector.tensor_copy(T.p[:], T.acc[:, 0:D]).then_inc(S.cp, 1)
     g.sync.wait_ge(S.cp, 1)
     g.sync.dma_start(T.stage[:], T.p[:]).then_inc(S.staged, 16)
+    if mine is not None:
+        g.scalar.wait_ge(S.cp, 1)
+        g.scalar.dma_start(T.own0[:], T.p[mine * W:(mine + 1) * W, :]).then_inc(S.owns, 16)
 
     g.wait_ge(S.staged, 16)
-    sent = 0
     trs = []
-    mine = None
-    for s, pair in enumerate(pairs):
-        if core in pair:
-            mine = s
-        dsts = [d for d in pair if d != core]
-        trs.append(RemoteDMATransfer(dst_ids=[dst_id(d) for d in dsts], dma_engine_mask=1 << engines[s],
-                                     remote_sem=S.arr, srcs=[T.stage[s]],
-                                     dsts=[T.land[slot(core, d)] for d in dsts], alu_op=0))
-        sent += 1
+    for s, d in enumerate(owners):
+        if d != core:
+            trs.append(RemoteDMATransfer(dst_ids=[dst_id(d)], dma_engine_mask=1 << engines[len(trs)],
+                                         remote_sem=S.arr, srcs=[T.stage[s]], dsts=[T.land[slot(core, d)]], alu_op=0))
     g.remote_dma_fused(trs, local_sem=S.sent)
+    sent = len(trs)
 
     if mine is not None:
-        g.wait_ge(S.arr, len(others))
-        dsts = [d for d in others if topo.mates(core, d) or topo.same_plane(core, d)]
-        g.remote_dma_fused([RemoteDMATransfer(dst_ids=[dst_id(d) for d in dsts], dma_engine_mask=all_mask,
+        g.wait_ge(S.arr, NO)
+        g.remote_dma_fused([RemoteDMATransfer(dst_ids=[dst_id(d) for d in others], dma_engine_mask=allowed,
                                               remote_sem=S.got,
-                                              srcs=[T.stage[mine]] + [T.land[i] for i in range(len(others))],
-                                              dsts=[T.res[mine] for d in dsts], alu_op=1)], local_sem=S.sent)
+                                              srcs=[T.stage[mine]] + [T.land[i] for i in range(NO)],
+                                              dsts=[T.res[mine] for d in others], alu_op=1)], local_sem=S.sent)
         sent += len(engines)
+        g.scalar.wait_ge(S.arr, NO)
+        g.scalar.dma_start(T.lz[:], T.land[:]).then_inc(S.lzs, 16)
+        g.tensor.wait_ge(S.sels, 16)
+        g.tensor.wait_ge(S.lzs, 16)
+        g.tensor.matmul(T.acc2[0:W, 0:D], T.sel[:], T.lz[:], True, True).then_inc(S.sm, 1)
+        g.vector.wait_ge(S.owns, 16)
+        g.vector.wait_ge(S.sm, 1)
+        g.vector.tensor_tensor(T.ysl[:], T.acc2[0:W, 0:D], T.own0[:], AluOpType.add).then_inc(S.ys, 1)
+        g.scalar.wait_ge(S.ys, 1)
+        g.scalar.dma_start(T.y[mine * W:(mine + 1) * W, :], T.ysl[:]).then_inc(S.doneo, 16)
 
-    g.sync.wait_ge(S.got, K * len(engines))
-    g.sync.dma_start(T.y[:], T.res[:]).then_inc(S.done, 16)
-    g.sync.wait_ge(S.done, 16)
+    n_in = NP - (0 if mine is None else 1)
+    g.sync.wait_ge(S.got, n_in * len(engines))
+    done = 0
+    if mine is None:
+        g.sync.dma_start(T.y[:], T.res[:]).then_inc(S.done, 16)
+        done += 16
+    else:
+        if mine > 0:
+            g.sync.dma_start(T.y[0:mine * W, :], T.res[0:mine]).then_inc(S.done, 16)
+            done += 16
+        if mine < NP - 1:
+            g.sync.dma_start(T.y[(mine + 1) * W:D, :], T.res[mine + 1:NP]).then_inc(S.done, 16)
+            done += 16
+        g.scalar.wait_ge(S.doneo, 16)
+    g.sync.wait_ge(S.done, done)
     g.wait_ge(S.sent, sent)

import comms_topo
from concourse.bass import DstId, RemoteDMATransfer
from concourse.mybir import AluOpType

CORES = [6, 14, 22, 30, 38, 134, 142, 150, 158]
D = 128


def _owners(cores, topo):
    return [a for a in cores if any(topo.mates(a, b) for b in cores)]


NP = len(_owners(CORES, comms_topo))
W = D // NP
NO = len(CORES) - 1

SCRATCH = {
    "sah": ("sbuf", [D, D], "bfloat16"),
    "sal": ("sbuf", [D, D], "bfloat16"),
    "sbh": ("sbuf", [D, D], "bfloat16"),
    "sbl": ("sbuf", [D, D], "bfloat16"),
    "acc": ("psum", [D, 512], "float32"),
    "acc2": ("psum", [D, 512], "float32"),
    "p": ("sbuf", [D, D], "float32"),
    "stage": ("dram", [NP, D, W], "float32"),
    "land": ("dram", [NO, D, W], "float32"),
    "res": ("dram", [NP, D, W], "float32"),
    "u": ("sbuf", [D, W + 1], "float32"),
    "zdd": ("dram", [NO, W * (W + 1)], "float32"),
    "sel": ("sbuf", [D, W], "float32"),
    "lz": ("sbuf", [D, D], "float32"),
    "own0": ("sbuf", [W, D], "float32"),
    "ysl": ("sbuf", [W, D], "float32"),
}
SEMAPHORES = ["ldh", "ldl", "mm", "cp", "staged", "arr", "sent", "got", "done",
              "ms", "zs", "sels", "owns", "lzs", "sm", "ys", "doneo"]


def rank_program(g, core, T, topo):
    rank = T.rank_of(core)
    if rank is None:
        return
    S = T.sem
    cores = list(T.cores)
    others = [c for c in cores if c != core]
    owners = _owners(cores, topo)
    mine = owners.index(core) if core in owners else None

    def dst_id(d):
        rid, pid = topo.addr(d, core)
        return DstId(rid=rid, pnc=pid)

    def slot(sender, receiver):
        a, b = T.rank_of(sender), T.rank_of(receiver)
        return a - (1 if a > b else 0)

    allowed = topo.mask(core, others[0])
    for d in others:
        allowed &= topo.mask(core, d)
    engines = [e for e in range(16) if (allowed >> e) & 1]

    g.sync.dma_start(T.sah[:], T.ah[:]).then_inc(S.ldh, 16)
    g.scalar.dma_start(T.sbh[:], T.bh[:]).then_inc(S.ldh, 16)
    g.sync.dma_start(T.sal[:], T.al[:]).then_inc(S.ldl, 16)
    g.scalar.dma_start(T.sbl[:], T.bl[:]).then_inc(S.ldl, 16)
    if mine is not None:
        g.vector.memset(T.u[:], 0.0).then_inc(S.ms, 1)
        g.vector.wait_ge(S.ms, 1)
        g.vector.memset(T.u[:, 0:1], 1.0).then_inc(S.ms, 1)
        g.scalar.wait_ge(S.ms, 2)
        g.scalar.dma_start(T.zdd[:], T.u[:]).then_inc(S.zs, 16)
        g.scalar.wait_ge(S.zs, 16)
        g.scalar.dma_start(T.sel[:], T.zdd[:, 0:W * W]).then_inc(S.sels, 16)
    g.tensor.wait_ge(S.ldh, 32)
    g.tensor.matmul(T.acc[:, 0:D], T.sah[:], T.sbh[:], True, False).then_inc(S.mm, 1)
    g.tensor.wait_ge(S.ldl, 32)
    g.tensor.matmul(T.acc[:, 0:D], T.sah[:], T.sbl[:], False, False).then_inc(S.mm, 1)
    g.tensor.matmul(T.acc[:, 0:D], T.sal[:], T.sbh[:], False, False).then_inc(S.mm, 1)
    g.tensor.matmul(T.acc[:, 0:D], T.sal[:], T.sbl[:], False, True).then_inc(S.mm, 1)

    g.vector.wait_ge(S.mm, 4)
    g.vector.tensor_copy(T.p[:], T.acc[:, 0:D]).then_inc(S.cp, 1)
    g.sync.wait_ge(S.cp, 1)
    g.sync.dma_start(T.stage[:], T.p[:]).then_inc(S.staged, 16)
    if mine is not None:
        g.scalar.wait_ge(S.cp, 1)
        g.scalar.dma_start(T.own0[:], T.p[mine * W:(mine + 1) * W, :]).then_inc(S.owns, 16)

    g.wait_ge(S.staged, 16)
    trs = []
    for s, d in enumerate(owners):
        if d != core:
            trs.append(RemoteDMATransfer(dst_ids=[dst_id(d)], dma_engine_mask=1 << engines[len(trs)],
                                         remote_sem=S.arr, srcs=[T.stage[s]], dsts=[T.land[slot(core, d)]], alu_op=0))
    g.remote_dma_fused(trs, local_sem=S.sent)
    sent = len(trs)

    if mine is not None:
        g.wait_ge(S.arr, NO)
        g.remote_dma_fused([RemoteDMATransfer(dst_ids=[dst_id(d) for d in others], dma_engine_mask=allowed,
                                              remote_sem=S.got,
                                              srcs=[T.stage[mine]] + [T.land[i] for i in range(NO)],
                                              dsts=[T.res[mine] for d in others], alu_op=1)], local_sem=S.sent)
        sent += len(engines)
        g.scalar.wait_ge(S.arr, NO)
        g.scalar.dma_start(T.lz[:], T.land[:]).then_inc(S.lzs, 16)
        g.tensor.wait_ge(S.sels, 16)
        g.tensor.wait_ge(S.lzs, 16)
        g.tensor.matmul(T.acc2[0:W, 0:D], T.sel[:], T.lz[:], True, True).then_inc(S.sm, 1)
        g.vector.wait_ge(S.owns, 16)
        g.vector.wait_ge(S.sm, 1)
        g.vector.tensor_tensor(T.ysl[:], T.acc2[0:W, 0:D], T.own0[:], AluOpType.add).then_inc(S.ys, 1)
        g.scalar.wait_ge(S.ys, 1)
        g.scalar.dma_start(T.y[mine * W:(mine + 1) * W, :], T.ysl[:]).then_inc(S.doneo, 16)

    n_in = NP - (0 if mine is None else 1)
    g.sync.wait_ge(S.got, n_in * len(engines))
    done = 0
    if mine is None:
        g.sync.dma_start(T.y[:], T.res[:]).then_inc(S.done, 16)
        done += 16
    else:
        if mine > 0:
            g.sync.dma_start(T.y[0:mine * W, :], T.res[0:mine]).then_inc(S.done, 16)
            done += 16
        if mine < NP - 1:
            g.sync.dma_start(T.y[(mine + 1) * W:D, :], T.res[mine + 1:NP]).then_inc(S.done, 16)
            done += 16
        g.scalar.wait_ge(S.doneo, 16)
    g.sync.wait_ge(S.done, done)
    g.wait_ge(S.sent, sent)
